import numpy as np
import ml_dtypes


def mxq(x, axis, fmt="e4m3"):
    dtype, down = {"e4m3": (ml_dtypes.float8_e4m3fn, 7), "e5m2": (ml_dtypes.float8_e5m2, 14)}[fmt]
    v = np.moveaxis(np.asarray(x, np.float32).astype(ml_dtypes.bfloat16).astype(np.float64), axis, -1)
    blocks = v.reshape(v.shape[:-1] + (-1, 32))
    amax = np.abs(blocks).max(-1, keepdims=True)
    byte = np.maximum(np.where(amax > 0, np.frexp(amax)[1] - 1 + 127, 0) - down, 1)
    scale = np.exp2(byte - 127.0)
    codes = (blocks / scale).astype(np.float32).astype(dtype).astype(np.float64)
    return np.moveaxis((codes * scale).reshape(v.shape), -1, axis)


WIDE = False


def mx_kscale(k):
    if not WIDE:
        return np.ones(k)
    levels = np.array([10, -10, 5, -5, 0])
    if k % 512:
        return np.exp2(np.random.permutation(np.resize(levels, k // 32))).repeat(32)
    a = np.empty((k // 512, 16))
    for p in range(k // 512):
        a[p, :8] = np.random.permutation(np.resize(levels, 8))
        for g in range(8):
            far = levels[np.abs(levels - a[p, g]) >= 10]
            a[p, g + 8] = far[np.random.randint(len(far))]
    return np.exp2(a.ravel()).repeat(32)


def f64(x):
    return np.asarray(x).astype(np.float64)


def striped8(idx):
    return np.asarray(idx).reshape(8, -1, 16).transpose(0, 2, 1).reshape(128, -1).astype(np.uint16)


def unstriped8(offs):
    return offs.reshape(8, 16, -1).transpose(0, 2, 1).reshape(8, -1).astype(np.int64)


def pick8(x, idx, run):
    r = np.arange(len(x))
    return x[r[:, None], idx[r % (8 * run) // run]]


E2M1 = np.array([0.0, 0.5, 1.0, 1.5, 2.0, 3.0, 4.0, 6.0, -0.0, -0.5, -1.0, -1.5, -2.0, -3.0, -4.0, -6.0])


def pack_weight(w, fmt):
    k, n = w.shape
    w = f64(np.asarray(w, np.float32).astype(ml_dtypes.bfloat16)).reshape(k // 32, 32, n)
    amax = np.abs(w).max(1)
    if fmt == "e4m3":
        byte = np.frexp(amax)[1] - 1 + 127 - 7
    else:
        mant, ex = np.frexp(amax / 6.0)
        byte = np.where(mant > 0.5, ex, ex - 1) + 127
    byte = np.clip(np.where(amax > 0, byte, 1), 1, 254)
    scaled = (w * np.exp2(127.0 - byte)[:, None, :]).reshape(k, n).astype(np.float32)
    by_word = np.ascontiguousarray(scaled.reshape(k // 512, 128, 4, n).transpose(0, 1, 3, 2))
    if fmt == "e4m3":
        words = by_word.astype(ml_dtypes.float8_e4m3fn).view(np.uint8)
    else:
        c = by_word.astype(ml_dtypes.float4_e2m1fn).view(np.uint8) & 0xF
        words = (c[..., 0::2] | (c[..., 1::2] << 4)).reshape(k // 512, 128, 2 * n)
    return np.ascontiguousarray(words), np.ascontiguousarray(byte.astype(np.uint8).reshape(k // 512, 16, n))


def unpack_weight(words, scales, fmt):
    g, _, n = scales.shape
    words = np.ascontiguousarray(words).reshape(g, 128, n, -1)
    if fmt == "e4m3":
        vals = words.view(ml_dtypes.float8_e4m3fn).astype(np.float64)
    else:
        nib = np.empty((g, 128, n, 4), np.uint8)
        nib[..., 0::2] = words & 0xF
        nib[..., 1::2] = words >> 4
        vals = E2M1[nib]
    vals = vals * np.repeat(np.exp2(scales.astype(np.float64) - 127.0), 8, axis=1)[..., None]
    return vals.transpose(0, 1, 3, 2).reshape(g * 512, n)


D, T, U, I, J, P, Q = 512, 1024, 1024, 256, 512, 512, 128


def setup_inputs():
    n = np.random.standard_normal
    idx = np.stack([np.random.permutation(U)[:I] for _ in range(8)])
    idx2 = np.stack([np.random.permutation(U)[:I] for _ in range(8)])
    idx3 = np.stack([np.random.permutation(P)[:I] for _ in range(8)])
    idx4 = np.stack([np.random.permutation(T)[:J] for _ in range(8)])
    idx5 = np.stack([np.random.permutation(T)[:J] for _ in range(8)])
    fd = mx_kscale(D)
    cachep = pack_weight(n((D, T)) / fd[:, None], "e4m3")
    draftp = pack_weight(n((D, U)) / fd[:, None], "e2m1")
    return {
        "query": (n((D, Q)) * 1.0 / np.sqrt(D) * fd[:, None]).astype(np.float32),
        "cache_words": cachep[0],
        "cache_scales": cachep[1],
        "draft_words": draftp[0],
        "draft_scales": draftp[1],
        "offs": striped8(idx),
        "offs2": striped8(idx2),
        "offs3": striped8(idx3),
        "offs4": striped8(idx4),
        "offs5": striped8(idx5),
    }


def reference(query, cache_words, cache_scales, draft_words, draft_scales, offs, offs2, offs3, offs4, offs5):
    idx = unstriped8(offs)
    idx2 = unstriped8(offs2)
    idx3 = unstriped8(offs3)
    idx4 = unstriped8(offs4)
    idx5 = unstriped8(offs5)
    cacheu = unpack_weight(cache_words, cache_scales, "e4m3")
    draftu = unpack_weight(draft_words, draft_scales, "e2m1")
    queryq = mxq(f64(query), 0, "e4m3")
    a = queryq.T @ cacheu
    b = queryq.T @ draftu
    pm = a.reshape(Q, P, T // P).sum(axis=2)
    w = pick8(b, idx, 16) - pick8(b, idx2, 16)
    f1 = np.zeros((Q, P))
    f1[np.arange(Q)[:, None], idx3[np.arange(Q) % 128 // 16]] = w
    m1 = np.maximum(f1, pm)
    sp = np.repeat(m1, T // P, axis=1)
    r = sp - a
    y = np.maximum(pick8(r, idx4, 16), pick8(a, idx5, 16))
    return y

@@ -1,0 +1,149 @@
+from contextlib import ExitStack
+
+import concourse.mybir as mybir
+
+D, T, U, I, J, PAGES, Q = 512, 1024, 1024, 256, 512, 512, 128
+FLOPS = 2 * Q * D * (T + U)
+
+F32 = mybir.dt.float32
+BF16 = mybir.dt.bfloat16
+I32 = mybir.dt.int32
+U32 = mybir.dt.uint32
+U16 = mybir.dt.uint16
+U8 = mybir.dt.uint8
+FP8X4 = mybir.dt.float8_e4m3fn_x4
+FP4X4 = mybir.dt.float4_e2m1fn_x4
+ALU = mybir.AluOpType
+COPY = mybir.ActivationFunctionType.Copy
+
+P = 128
+PACK = 4
+BANK = 512
+B_PASS = 256
+
+
+def tile_attend_tokenstopages_two_kernel(
+    tc, query, cache_words, cache_scales, draft_words, draft_scales, offs, offs2, offs3, offs4, offs5, out
+):
+    nc = tc.nc
+    with ExitStack() as ctx:
+        lists = ctx.enter_context(tc.tile_pool(name="lists", bufs=1))
+        sb = ctx.enter_context(tc.tile_pool(name="sb", bufs=1))
+        ps = ctx.enter_context(tc.psum_pool(name="ps", bufs=1))
+
+        def load_scales(queue, plane, rows):
+            for quad in range(4):
+                queue.dma_start(
+                    out=plane[32 * quad : 32 * quad + 4, :].bitcast(I32),
+                    in_=rows[0, 4 * quad : 4 * quad + 4, :].bitcast(I32),
+                )
+
+        def load_list(src, name):
+            tile = lists.tile([P, src.shape[1]], U16, name=name)
+            nc.sync.dma_start(tile[:], src)
+            return tile
+
+        d_plane = sb.tile([P, U], U8, align_bytes=64)
+        c_plane = sb.tile([P, T], U8, align_bytes=64)
+        f1 = sb.tile([P, PAGES], F32)
+        nc.vector.memset(d_plane[:].bitcast(I32), 0)
+        nc.gpsimd.memset(c_plane[:].bitcast(I32), 0)
+
+        q_raw = sb.tile([P, PACK, Q], F32)
+        nc.sync.dma_start(out=q_raw[:], in_=query.rearrange("(p j) q -> p j q", j=PACK))
+        load_scales(nc.sync, d_plane, draft_scales)
+        d_words = sb.tile([P, 2 * U], U8, align_bytes=64)
+        nc.sync.dma_start(out=d_words[:].bitcast(I32), in_=draft_words[0].bitcast(I32))
+        l1 = load_list(offs, "l1")
+        l2 = load_list(offs2, "l2")
+        load_scales(nc.sync, c_plane, cache_scales)
+        c_words = sb.tile([P, T], I32, align_bytes=64)
+        nc.sync.dma_start(out=c_words[:], in_=cache_words[0].rearrange("p n t -> p (n t)").bitcast(I32))
+        l3 = load_list(offs3, "l3")
+        l5 = load_list(offs5, "l5")
+        l4 = load_list(offs4, "l4")
+        nc.vector.memset(f1[:], 0.0)
+
+        q_bf = sb.tile([P, Q, PACK], BF16, align_bytes=64)
+        nc.vector.tensor_copy(
+            out=q_bf[:].rearrange("p (c i) j -> p c j i", i=4),
+            in_=q_raw[:].rearrange("p j (c i) -> p c j i", i=4),
+        )
+        q_codes = sb.tile([P, Q], U32, align_bytes=64)
+        q_plane = sb.tile([P, Q], U8, align_bytes=64)
+        nc.vector.quantize_mx(
+            out=q_codes[:].bitcast(FP8X4), scales=q_plane[:], in_=q_bf[:].rearrange("p q j -> p (q j)")
+        )
+
+        b_sb = sb.tile([P, U], F32)
+        for n in range(U // B_PASS):
+            cols = slice(n * B_PASS, (n + 1) * B_PASS)
+            b_ps = ps.tile([P, B_PASS], F32, name=f"b_ps{n}")
+            nc.tensor.matmul_mx(
+                out=b_ps[:],
+                lhsT=q_codes[:].bitcast(FP8X4),
+                lhsT_scale=q_plane[:],
+                rhs=d_words[:, 2 * n * B_PASS : 2 * (n + 1) * B_PASS].bitcast(FP4X4),
+                rhs_scale=d_plane[:, cols],
+                start=True,
+                stop=True,
+            )
+            if n % 2 == 0:
+                nc.scalar.activation(b_sb[:, cols], b_ps[:], COPY)
+            else:
+                nc.vector.tensor_copy(b_sb[:, cols], b_ps[:])
+
+        a_ps = []
+        for n in range(T // BANK):
+            cols = slice(n * BANK, (n + 1) * BANK)
+            bank = ps.tile([P, BANK], F32, name=f"a_ps{n}")
+            nc.tensor.matmul_mx(
+                out=bank[:],
+                lhsT=q_codes[:].bitcast(FP8X4),
+                lhsT_scale=q_plane[:],
+                rhs=c_words[:, cols].bitcast(FP8X4),
+                rhs_scale=c_plane[:, cols],
+                start=True,
+                stop=True,
+            )
+            a_ps.append(bank)
+
+        b1 = sb.tile([P, I], F32)
+        b2 = sb.tile([P, I], F32)
+        w = sb.tile([P, I], F32)
+        nc.scalar.activation(b1[:], b_sb[:].indirect(l1[:]), COPY)
+        nc.vector.tensor_copy(b2[:], b_sb[:].indirect(l2[:]))
+        nc.vector.tensor_tensor(w[:], b1[:], b2[:], ALU.subtract)
+        nc.scalar.activation(f1[:].indirect(l3[:]), w[:], COPY)
+
+        a_sb = sb.tile([P, T], F32)
+        for n in range(T // BANK):
+            nc.vector.tensor_copy(a_sb[:, n * BANK : (n + 1) * BANK], a_ps[n][:])
+        pm = sb.tile([P, PAGES], F32)
+        pairs = a_sb[:].rearrange("p (g e) -> p g e", e=2)
+        nc.vector.tensor_tensor(pm[:], pairs[:, :, 0], pairs[:, :, 1], ALU.add)
+
+        a5 = sb.tile([P, J], F32)
+        nc.scalar.activation(a5[:], a_sb[:].indirect(l5[:]), COPY)
+
+        m1 = sb.tile([P, PAGES], F32)
+        nc.vector.tensor_tensor(m1[:], f1[:], pm[:], ALU.max)
+        r = sb.tile([P, T], F32)
+        nc.vector.tensor_tensor(
+            r[:].rearrange("p (g e) -> p g e", e=2),
+            m1[:].unsqueeze(2).to_broadcast([P, PAGES, 2]),
+            pairs,
+            ALU.subtract,
+        )
+
+        half = J // 2
+        r4a = sb.tile([P, half], F32)
+        r4b = sb.tile([P, half], F32)
+        nc.vector.tensor_copy(r4a[:], r[:].indirect(l4[:, : half // 16]))
+        nc.scalar.activation(r4b[:], r[:].indirect(l4[:, half // 16 :]), COPY)
+        yb = sb.tile([P, half], F32)
+        ya = sb.tile([P, half], F32)
+        nc.vector.tensor_tensor(yb[:], r4b[:], a5[:, half:], ALU.max)
+        nc.sync.dma_start(out=out[:, half:], in_=yb[:])
+        nc.vector.tensor_tensor(ya[:], r4a[:], a5[:, :half], ALU.max)
+        nc.scalar.dma_start(out=out[:, :half], in_=ya[:])

@@ -19,7 +19,8 @@ COPY = mybir.ActivationFunctionType.Copy
 P = 128
 PACK = 4
 BANK = 512
-B_PASS = 256
+SPLIT = 320
+B_PASSES = (512, 256, 128, 128)
 
 
 def tile_attend_tokenstopages_two_kernel(
@@ -47,51 +48,59 @@ def tile_attend_tokenstopages_two_kernel(
         c_plane = sb.tile([P, T], U8, align_bytes=64)
         f1 = sb.tile([P, PAGES], F32)
         nc.vector.memset(d_plane[:].bitcast(I32), 0)
-        nc.gpsimd.memset(c_plane[:].bitcast(I32), 0)
+        nc.vector.memset(c_plane[:].bitcast(I32), 0)
 
         q_raw = sb.tile([P, PACK, Q], F32)
         nc.sync.dma_start(out=q_raw[:], in_=query.rearrange("(p j) q -> p j q", j=PACK))
-        load_scales(nc.sync, d_plane, draft_scales)
         d_words = sb.tile([P, 2 * U], U8, align_bytes=64)
-        nc.sync.dma_start(out=d_words[:].bitcast(I32), in_=draft_words[0].bitcast(I32))
+        nc.sync.dma_start(out=d_words[:, :U].bitcast(I32), in_=draft_words[0, :, :U].bitcast(I32))
+        load_scales(nc.sync, d_plane, draft_scales)
+        nc.sync.dma_start(out=d_words[:, U:].bitcast(I32), in_=draft_words[0, :, U:].bitcast(I32))
+        c_words = sb.tile([P, T], I32, align_bytes=64)
+        nc.sync.dma_start(out=c_words[:], in_=cache_words[0].rearrange("p n t -> p (n t)").bitcast(I32))
         l1 = load_list(offs, "l1")
         l2 = load_list(offs2, "l2")
         load_scales(nc.sync, c_plane, cache_scales)
-        c_words = sb.tile([P, T], I32, align_bytes=64)
-        nc.sync.dma_start(out=c_words[:], in_=cache_words[0].rearrange("p n t -> p (n t)").bitcast(I32))
         l3 = load_list(offs3, "l3")
         l5 = load_list(offs5, "l5")
         l4 = load_list(offs4, "l4")
         nc.vector.memset(f1[:], 0.0)
 
         q_bf = sb.tile([P, Q, PACK], BF16, align_bytes=64)
-        nc.vector.tensor_copy(
-            out=q_bf[:].rearrange("p (c i) j -> p c j i", i=4),
-            in_=q_raw[:].rearrange("p j (c i) -> p c j i", i=4),
-        )
         q_codes = sb.tile([P, Q], U32, align_bytes=64)
         q_plane = sb.tile([P, Q], U8, align_bytes=64)
-        nc.vector.quantize_mx(
-            out=q_codes[:].bitcast(FP8X4), scales=q_plane[:], in_=q_bf[:].rearrange("p q j -> p (q j)")
-        )
+        q_halves = [slice(0, Q // 2), slice(Q // 2, Q)]
+        for rows in q_halves:
+            nc.vector.tensor_copy(
+                out=q_bf[:, rows, :].rearrange("p (c i) j -> p c j i", i=4),
+                in_=q_raw[:, :, rows].rearrange("p j (c i) -> p c j i", i=4),
+            )
+        for rows in q_halves:
+            nc.vector.quantize_mx(
+                out=q_codes[:, rows].bitcast(FP8X4),
+                scales=q_plane[:, rows],
+                in_=q_bf[:, rows, :].rearrange("p q j -> p (q j)"),
+            )
 
-        b_sb = sb.tile([P, U], F32)
-        for n in range(U // B_PASS):
-            cols = slice(n * B_PASS, (n + 1) * B_PASS)
-            b_ps = ps.tile([P, B_PASS], F32, name=f"b_ps{n}")
+        b_sb = sb.tile([P, U], F32, tag="scores")
+        first = 0
+        for n, width in enumerate(B_PASSES):
+            cols = slice(first, first + width)
+            b_ps = ps.tile([P, width], F32, name=f"b_ps{n}")
             nc.tensor.matmul_mx(
                 out=b_ps[:],
                 lhsT=q_codes[:].bitcast(FP8X4),
                 lhsT_scale=q_plane[:],
-                rhs=d_words[:, 2 * n * B_PASS : 2 * (n + 1) * B_PASS].bitcast(FP4X4),
+                rhs=d_words[:, 2 * first : 2 * (first + width)].bitcast(FP4X4),
                 rhs_scale=d_plane[:, cols],
                 start=True,
                 stop=True,
             )
-            if n % 2 == 0:
+            if n in (0, 3):
                 nc.scalar.activation(b_sb[:, cols], b_ps[:], COPY)
             else:
                 nc.vector.tensor_copy(b_sb[:, cols], b_ps[:])
+            first += width
 
         a_ps = []
         for n in range(T // BANK):
@@ -114,29 +123,39 @@ def tile_attend_tokenstopages_two_kernel(
         nc.scalar.activation(b1[:], b_sb[:].indirect(l1[:]), COPY)
         nc.vector.tensor_copy(b2[:], b_sb[:].indirect(l2[:]))
         nc.vector.tensor_tensor(w[:], b1[:], b2[:], ALU.subtract)
+        a_sb = sb.tile([P, T], F32, tag="scores")
         nc.scalar.activation(f1[:].indirect(l3[:]), w[:], COPY)
 
-        a_sb = sb.tile([P, T], F32)
         for n in range(T // BANK):
             nc.vector.tensor_copy(a_sb[:, n * BANK : (n + 1) * BANK], a_ps[n][:])
         pm = sb.tile([P, PAGES], F32)
         pairs = a_sb[:].rearrange("p (g e) -> p g e", e=2)
-        nc.vector.tensor_tensor(pm[:], pairs[:, :, 0], pairs[:, :, 1], ALU.add)
+        halves = [slice(n * PAGES // 2, (n + 1) * PAGES // 2) for n in range(2)]
+        for pages in halves:
+            nc.vector.tensor_tensor(pm[:, pages], pairs[:, pages, 0], pairs[:, pages, 1], ALU.add)
 
+        half = J // 2
         a5 = sb.tile([P, J], F32)
         nc.scalar.activation(a5[:], a_sb[:].indirect(l5[:]), COPY)
 
         m1 = sb.tile([P, PAGES], F32)
-        nc.vector.tensor_tensor(m1[:], f1[:], pm[:], ALU.max)
+        for pages in halves:
+            nc.vector.tensor_tensor(m1[:, pages], f1[:, pages], pm[:, pages], ALU.max)
         r = sb.tile([P, T], F32)
-        nc.vector.tensor_tensor(
-            r[:].rearrange("p (g e) -> p g e", e=2),
-            m1[:].unsqueeze(2).to_broadcast([P, PAGES, 2]),
-            pairs,
-            ALU.subtract,
-        )
 
-        half = J // 2
+        def subtract_scores(engine, first, last, scores):
+            count = (last - first) // 2
+            engine.tensor_tensor(
+                r[:, first:last].rearrange("p (g e) -> p g e", e=2),
+                m1[:, first // 2 : last // 2].unsqueeze(2).to_broadcast([P, count, 2]),
+                scores.rearrange("p (g e) -> p g e", e=2),
+                ALU.subtract,
+            )
+
+        subtract_scores(nc.gpsimd, 0, SPLIT, a_sb[:, :SPLIT])
+        subtract_scores(nc.vector, SPLIT, BANK, a_ps[0][:, SPLIT:])
+        subtract_scores(nc.vector, BANK, T, a_ps[1][:])
+
         r4a = sb.tile([P, half], F32)
         r4b = sb.tile([P, half], F32)
         nc.vector.tensor_copy(r4a[:], r[:].indirect(l4[:, : half // 16]))
@@ -146,4 +165,4 @@ def tile_attend_tokenstopages_two_kernel(
         nc.vector.tensor_tensor(yb[:], r4b[:], a5[:, half:], ALU.max)
         nc.sync.dma_start(out=out[:, half:], in_=yb[:])
         nc.vector.tensor_tensor(ya[:], r4a[:], a5[:, :half], ALU.max)
-        nc.scalar.dma_start(out=out[:, :half], in_=ya[:])
+        nc.sync.dma_start(out=out[:, :half], in_=ya[:])

from contextlib import ExitStack

import concourse.mybir as mybir

D, T, U, I, J, PAGES, Q = 512, 1024, 1024, 256, 512, 512, 128
FLOPS = 2 * Q * D * (T + U)

F32 = mybir.dt.float32
BF16 = mybir.dt.bfloat16
I32 = mybir.dt.int32
U32 = mybir.dt.uint32
U16 = mybir.dt.uint16
U8 = mybir.dt.uint8
FP8X4 = mybir.dt.float8_e4m3fn_x4
FP4X4 = mybir.dt.float4_e2m1fn_x4
ALU = mybir.AluOpType
COPY = mybir.ActivationFunctionType.Copy

P = 128
PACK = 4
BANK = 512
SPLIT = 320
B_PASSES = (512, 256, 128, 128)


def tile_attend_tokenstopages_two_kernel(
    tc, query, cache_words, cache_scales, draft_words, draft_scales, offs, offs2, offs3, offs4, offs5, out
):
    nc = tc.nc
    with ExitStack() as ctx:
        lists = ctx.enter_context(tc.tile_pool(name="lists", bufs=1))
        sb = ctx.enter_context(tc.tile_pool(name="sb", bufs=1))
        ps = ctx.enter_context(tc.psum_pool(name="ps", bufs=1))

        def load_scales(queue, plane, rows):
            for quad in range(4):
                queue.dma_start(
                    out=plane[32 * quad : 32 * quad + 4, :].bitcast(I32),
                    in_=rows[0, 4 * quad : 4 * quad + 4, :].bitcast(I32),
                )

        def load_list(src, name):
            tile = lists.tile([P, src.shape[1]], U16, name=name)
            nc.sync.dma_start(tile[:], src)
            return tile

        d_plane = sb.tile([P, U], U8, align_bytes=64)
        c_plane = sb.tile([P, T], U8, align_bytes=64)
        f1 = sb.tile([P, PAGES], F32)
        nc.vector.memset(d_plane[:].bitcast(I32), 0)
        nc.vector.memset(c_plane[:].bitcast(I32), 0)

        q_raw = sb.tile([P, PACK, Q], F32)
        nc.sync.dma_start(out=q_raw[:], in_=query.rearrange("(p j) q -> p j q", j=PACK))
        d_words = sb.tile([P, 2 * U], U8, align_bytes=64)
        nc.sync.dma_start(out=d_words[:, :U].bitcast(I32), in_=draft_words[0, :, :U].bitcast(I32))
        load_scales(nc.sync, d_plane, draft_scales)
        nc.sync.dma_start(out=d_words[:, U:].bitcast(I32), in_=draft_words[0, :, U:].bitcast(I32))
        c_words = sb.tile([P, T], I32, align_bytes=64)
        nc.sync.dma_start(out=c_words[:], in_=cache_words[0].rearrange("p n t -> p (n t)").bitcast(I32))
        l1 = load_list(offs, "l1")
        l2 = load_list(offs2, "l2")
        load_scales(nc.sync, c_plane, cache_scales)
        l3 = load_list(offs3, "l3")
        l5 = load_list(offs5, "l5")
        l4 = load_list(offs4, "l4")
        nc.vector.memset(f1[:], 0.0)

        q_bf = sb.tile([P, Q, PACK], BF16, align_bytes=64)
        q_codes = sb.tile([P, Q], U32, align_bytes=64)
        q_plane = sb.tile([P, Q], U8, align_bytes=64)
        q_halves = [slice(0, Q // 2), slice(Q // 2, Q)]
        for rows in q_halves:
            nc.vector.tensor_copy(
                out=q_bf[:, rows, :].rearrange("p (c i) j -> p c j i", i=4),
                in_=q_raw[:, :, rows].rearrange("p j (c i) -> p c j i", i=4),
            )
        for rows in q_halves:
            nc.vector.quantize_mx(
                out=q_codes[:, rows].bitcast(FP8X4),
                scales=q_plane[:, rows],
                in_=q_bf[:, rows, :].rearrange("p q j -> p (q j)"),
            )

        b_sb = sb.tile([P, U], F32, tag="scores")
        first = 0
        for n, width in enumerate(B_PASSES):
            cols = slice(first, first + width)
            b_ps = ps.tile([P, width], F32, name=f"b_ps{n}")
            nc.tensor.matmul_mx(
                out=b_ps[:],
                lhsT=q_codes[:].bitcast(FP8X4),
                lhsT_scale=q_plane[:],
                rhs=d_words[:, 2 * first : 2 * (first + width)].bitcast(FP4X4),
                rhs_scale=d_plane[:, cols],
                start=True,
                stop=True,
            )
            if n in (0, 3):
                nc.scalar.activation(b_sb[:, cols], b_ps[:], COPY)
            else:
                nc.vector.tensor_copy(b_sb[:, cols], b_ps[:])
            first += width

        a_ps = []
        for n in range(T // BANK):
            cols = slice(n * BANK, (n + 1) * BANK)
            bank = ps.tile([P, BANK], F32, name=f"a_ps{n}")
            nc.tensor.matmul_mx(
                out=bank[:],
                lhsT=q_codes[:].bitcast(FP8X4),
                lhsT_scale=q_plane[:],
                rhs=c_words[:, cols].bitcast(FP8X4),
                rhs_scale=c_plane[:, cols],
                start=True,
                stop=True,
            )
            a_ps.append(bank)

        b1 = sb.tile([P, I], F32)
        b2 = sb.tile([P, I], F32)
        w = sb.tile([P, I], F32)
        nc.scalar.activation(b1[:], b_sb[:].indirect(l1[:]), COPY)
        nc.vector.tensor_copy(b2[:], b_sb[:].indirect(l2[:]))
        nc.vector.tensor_tensor(w[:], b1[:], b2[:], ALU.subtract)
        a_sb = sb.tile([P, T], F32, tag="scores")
        nc.scalar.activation(f1[:].indirect(l3[:]), w[:], COPY)

        for n in range(T // BANK):
            nc.vector.tensor_copy(a_sb[:, n * BANK : (n + 1) * BANK], a_ps[n][:])
        pm = sb.tile([P, PAGES], F32)
        pairs = a_sb[:].rearrange("p (g e) -> p g e", e=2)
        halves = [slice(n * PAGES // 2, (n + 1) * PAGES // 2) for n in range(2)]
        for pages in halves:
            nc.vector.tensor_tensor(pm[:, pages], pairs[:, pages, 0], pairs[:, pages, 1], ALU.add)

        half = J // 2
        a5 = sb.tile([P, J], F32)
        nc.scalar.activation(a5[:], a_sb[:].indirect(l5[:]), COPY)

        m1 = sb.tile([P, PAGES], F32)
        for pages in halves:
            nc.vector.tensor_tensor(m1[:, pages], f1[:, pages], pm[:, pages], ALU.max)
        r = sb.tile([P, T], F32)

        def subtract_scores(engine, first, last, scores):
            count = (last - first) // 2
            engine.tensor_tensor(
                r[:, first:last].rearrange("p (g e) -> p g e", e=2),
                m1[:, first // 2 : last // 2].unsqueeze(2).to_broadcast([P, count, 2]),
                scores.rearrange("p (g e) -> p g e", e=2),
                ALU.subtract,
            )

        subtract_scores(nc.gpsimd, 0, SPLIT, a_sb[:, :SPLIT])
        subtract_scores(nc.vector, SPLIT, BANK, a_ps[0][:, SPLIT:])
        subtract_scores(nc.vector, BANK, T, a_ps[1][:])

        r4a = sb.tile([P, half], F32)
        r4b = sb.tile([P, half], F32)
        nc.vector.tensor_copy(r4a[:], r[:].indirect(l4[:, : half // 16]))
        nc.scalar.activation(r4b[:], r[:].indirect(l4[:, half // 16 :]), COPY)
        yb = sb.tile([P, half], F32)
        ya = sb.tile([P, half], F32)
        nc.vector.tensor_tensor(yb[:], r4b[:], a5[:, half:], ALU.max)
        nc.sync.dma_start(out=out[:, half:], in_=yb[:])
        nc.vector.tensor_tensor(ya[:], r4a[:], a5[:, :half], ALU.max)
        nc.sync.dma_start(out=out[:, :half], in_=ya[:])
